import numpy as np
import ml_dtypes


def mxq(x, axis, fmt="e4m3"):
    dtype, down = {"e4m3": (ml_dtypes.float8_e4m3fn, 7), "e5m2": (ml_dtypes.float8_e5m2, 14)}[fmt]
    v = np.moveaxis(np.asarray(x, np.float32).astype(ml_dtypes.bfloat16).astype(np.float64), axis, -1)
    blocks = v.reshape(v.shape[:-1] + (-1, 32))
    amax = np.abs(blocks).max(-1, keepdims=True)
    byte = np.maximum(np.where(amax > 0, np.frexp(amax)[1] - 1 + 127, 0) - down, 1)
    scale = np.exp2(byte - 127.0)
    codes = (blocks / scale).astype(np.float32).astype(dtype).astype(np.float64)
    return np.moveaxis((codes * scale).reshape(v.shape), -1, axis)


WIDE = False


def mx_kscale(k):
    if not WIDE:
        return np.ones(k)
    levels = np.array([10, -10, 5, -5, 0])
    if k % 512:
        return np.exp2(np.random.permutation(np.resize(levels, k // 32))).repeat(32)
    a = np.empty((k // 512, 16))
    for p in range(k // 512):
        a[p, :8] = np.random.permutation(np.resize(levels, 8))
        for g in range(8):
            far = levels[np.abs(levels - a[p, g]) >= 10]
            a[p, g + 8] = far[np.random.randint(len(far))]
    return np.exp2(a.ravel()).repeat(32)


def f64(x):
    return np.asarray(x).astype(np.float64)


def striped(idx):
    return np.tile(np.asarray(idx).reshape(-1, 16).T, (8, 1)).astype(np.uint16)


def unstriped(offs):
    return offs[:16].T.reshape(-1).astype(np.int64)


E2M1 = np.array([0.0, 0.5, 1.0, 1.5, 2.0, 3.0, 4.0, 6.0, -0.0, -0.5, -1.0, -1.5, -2.0, -3.0, -4.0, -6.0])


def pack_weight(w, fmt):
    k, n = w.shape
    w = f64(np.asarray(w, np.float32).astype(ml_dtypes.bfloat16)).reshape(k // 32, 32, n)
    amax = np.abs(w).max(1)
    if fmt == "e4m3":
        byte = np.frexp(amax)[1] - 1 + 127 - 7
    else:
        mant, ex = np.frexp(amax / 6.0)
        byte = np.where(mant > 0.5, ex, ex - 1) + 127
    byte = np.clip(np.where(amax > 0, byte, 1), 1, 254)
    scaled = (w * np.exp2(127.0 - byte)[:, None, :]).reshape(k, n).astype(np.float32)
    by_word = np.ascontiguousarray(scaled.reshape(k // 512, 128, 4, n).transpose(0, 1, 3, 2))
    if fmt == "e4m3":
        words = by_word.astype(ml_dtypes.float8_e4m3fn).view(np.uint8)
    else:
        c = by_word.astype(ml_dtypes.float4_e2m1fn).view(np.uint8) & 0xF
        words = (c[..., 0::2] | (c[..., 1::2] << 4)).reshape(k // 512, 128, 2 * n)
    return np.ascontiguousarray(words), np.ascontiguousarray(byte.astype(np.uint8).reshape(k // 512, 16, n))


def unpack_weight(words, scales, fmt):
    g, _, n = scales.shape
    words = np.ascontiguousarray(words).reshape(g, 128, n, -1)
    if fmt == "e4m3":
        vals = words.view(ml_dtypes.float8_e4m3fn).astype(np.float64)
    else:
        nib = np.empty((g, 128, n, 4), np.uint8)
        nib[..., 0::2] = words & 0xF
        nib[..., 1::2] = words >> 4
        vals = E2M1[nib]
    vals = vals * np.repeat(np.exp2(scales.astype(np.float64) - 127.0), 8, axis=1)[..., None]
    return vals.transpose(0, 1, 3, 2).reshape(g * 512, n)


D, E, T, I, G, U, Q = 512, 512, 2048, 1024, 64, 256, 128


def setup_inputs():
    n = np.random.standard_normal
    idx = np.random.permutation(T)[:I]
    idx2 = np.random.permutation(U)[:G]
    fd = mx_kscale(D)
    fe = mx_kscale(E)
    keysp = pack_weight(n((D, T)) / fd[:, None], "e4m3")
    valsp = pack_weight(n((E, T)) / fe[:, None], "e4m3")
    return {
        "query": (n((D, Q)) * 0.6 / np.sqrt(D) * fd[:, None]).astype(np.float32),
        "keys_words": keysp[0],
        "keys_scales": keysp[1],
        "pquery": (n((D, Q)) * 1.0 / np.sqrt(D) * fd[:, None]).astype(np.float32),
        "pgsum": (n((D, U)) / fd[:, None]).astype(np.float32),
        "gout": (n((E, Q)) * 1 / np.sqrt(E) * fe[:, None]).astype(np.float32),
        "vals_words": valsp[0],
        "vals_scales": valsp[1],
        "old": (0.1 * n((Q, T))).astype(np.float32),
        "offs": striped(idx),
        "offs2": striped(idx2),
    }


def reference(query, keys_words, keys_scales, pquery, pgsum, gout, vals_words, vals_scales, old, offs, offs2):
    idx = unstriped(offs)
    idx2 = unstriped(offs2)
    keysu = unpack_weight(keys_words, keys_scales, "e4m3")
    valsu = unpack_weight(vals_words, vals_scales, "e4m3")
    pqueryq = mxq(f64(pquery), 0, "e4m3")
    pgsumq = mxq(f64(pgsum), 0, "e4m3")
    b = pqueryq.T @ pgsumq
    pb = np.exp(b - np.max(b, axis=1, keepdims=True))
    mb = pb / np.sum(pb, axis=1, keepdims=True)
    queryq = mxq(f64(query), 0, "e4m3")
    keysidxg = keysu[:, idx]
    a = queryq.T @ keysidxg
    pa = np.exp(a - np.max(a, axis=1, keepdims=True))
    zi = 1.0 / pa.reshape(Q, G, I // G).sum(axis=2)
    zr = np.repeat(zi, I // G, axis=1)
    sh = pa * zr
    goutq = mxq(f64(gout), 0, "e4m3")
    valsidxg = valsu[:, idx]
    dp = goutq.T @ valsidxg
    md = (sh * dp).reshape(Q, G, I // G).sum(axis=2)
    mr = np.repeat(md, I // G, axis=1)
    mg = mb[:, idx2] * 256.0
    mgr = np.repeat(mg, I // G, axis=1)
    ds = sh * mgr * (dp - mr)
    df = np.zeros((Q, T))
    df[:, idx] = ds
    y = f64(old) + df
    return y

@@ -1,0 +1,185 @@
+from contextlib import ExitStack
+
+import concourse.mybir as mybir
+
+D, E, T, I, G, U, Q = 512, 512, 2048, 1024, 64, 256, 128
+FLOPS = 2 * Q * (D * U + D * I + E * I)
+
+F32 = mybir.dt.float32
+BF16 = mybir.dt.bfloat16
+I32 = mybir.dt.int32
+U32 = mybir.dt.uint32
+U16 = mybir.dt.uint16
+U8 = mybir.dt.uint8
+FP8X4 = mybir.dt.float8_e4m3fn_x4
+ALU = mybir.AluOpType
+ACT = mybir.ActivationFunctionType
+AX = mybir.AxisListType
+
+P = 128
+PACK = 4
+PAGE = I // G
+KCH = 512
+VCH = 256
+PER_PAGE = (False, False)
+
+
+def tile_attend_gwithinpage_kernel(tc, query, keys_words, keys_scales, pquery, pgsum, gout, vals_words, vals_scales, old, offs, offs2, out):
+    nc = tc.nc
+    with ExitStack() as ctx:
+        lists = ctx.enter_context(tc.tile_pool(name="lists", bufs=1))
+        sb = ctx.enter_context(tc.tile_pool(name="sb", bufs=1))
+        lap = ctx.enter_context(tc.tile_pool(name="lap", bufs=1))
+        ps = ctx.enter_context(tc.psum_pool(name="ps", bufs=1))
+
+        offs_t = lists.tile([P, I // 16], U16, name="offs_t")
+        offs2_t = lists.tile([P, G // 16], U16, name="offs2_t")
+
+        def load_raw(src, flat):
+            raw = flat.rearrange("p (j w) -> p j w", j=PACK)
+            nc.sync.dma_start(out=raw, in_=src.rearrange("(p j) w -> p j w", j=PACK))
+            return raw
+
+        def load_words(src, t):
+            nc.sync.dma_start(out=t[:].bitcast(I32), in_=src[0].rearrange("p n t -> p (n t)").bitcast(I32))
+
+        def load_scales(src, t, queue):
+            nc.vector.memset(t[:].bitcast(I32), 0)
+            for r in range(4):
+                queue.dma_start(out=t[r:P:32, :].bitcast(I32), in_=src[0, r:16:4, :].bitcast(I32))
+
+        def cast(raw, g):
+            nc.scalar.activation(out=g.rearrange("p (c i t) -> p c t i", i=4, t=PACK), in_=raw.rearrange("p t (c i) -> p c t i", i=4), func=ACT.Copy)
+
+        def quant(g, name):
+            width = g.shape[1] // PACK
+            codes = sb.tile([P, width], U32, name=name + "_c", align_bytes=64)
+            scales = sb.tile([P, width], U8, name=name + "_s", align_bytes=64)
+            nc.vector.quantize_mx(out=codes[:].bitcast(FP8X4), scales=scales[:], in_=g)
+            return codes, scales
+
+        def gather(t, window, lo, n):
+            nc.vector.tensor_copy(out=t[:], in_=window[:].indirect(offs_t[:, lo // 16:(lo + n) // 16]))
+
+        def mx(acc, lc, ls, rc, rs):
+            nc.tensor.matmul_mx(out=acc, lhsT=lc.bitcast(FP8X4), lhsT_scale=ls, rhs=rc.bitcast(FP8X4), rhs_scale=rs, start=True, stop=True)
+
+        nc.sync.dma_start(offs_t[:], offs)
+        raw0 = sb.tile([P, PACK * Q], F32, name="raw0", tag="raw")
+        q_raw = load_raw(query, raw0[:])
+        nc.sync.dma_start(offs2_t[:], offs2)
+        kw = sb.tile([P, T], U32, name="kw", tag="pool_a")
+        load_words(keys_words, kw)
+        ks = lap.tile([P, T], U8, name="ks", offset=1024)
+        load_scales(keys_scales, ks, nc.scalar)
+        vs = sb.tile([P, T], U8, name="vs")
+        load_scales(vals_scales, vs, nc.gpsimd)
+        df = sb.tile([P, T], F32, name="df")
+        nc.vector.memset(df[:], 0.0)
+
+        q_g = sb.tile([P, Q * PACK], BF16, name="q_g", tag="pool_b", align_bytes=64)
+        nc.vector.tensor_copy(out=q_g[:].rearrange("p (c i t) -> p c t i", i=4, t=PACK), in_=q_raw.rearrange("p t (c i) -> p c t i", i=4))
+        q_c, q_s = quant(q_g[:], "q")
+        raw1 = sb.tile([P, PACK * 2 * Q], F32, name="raw1", tag="raw")
+        pq_raw = load_raw(pquery, raw1[:, 0:PACK * Q])
+        go_raw = load_raw(gout, raw1[:, PACK * Q:])
+        raw2 = sb.tile([P, PACK * U], F32, name="raw2", tag="pool_b", align_bytes=64)
+        pg_raw = load_raw(pgsum, raw2[:])
+
+        two_g = sb.tile([P, PACK * 2 * Q], BF16, name="two_g", align_bytes=64)
+        pg_g = sb.tile([P, PACK * U], BF16, name="pg_g", align_bytes=64)
+        cast(pq_raw, two_g[:, 0:PACK * Q])
+        cast(go_raw, two_g[:, PACK * Q:])
+        cast(pg_raw, pg_g[:])
+
+        ksg = sb.tile([P, I], U8, name="ksg", align_bytes=64)
+        gather(ksg, ks, 0, I)
+        vw = lap.tile([P, T], U32, name="vw", offset=2048)
+        load_words(vals_words, vw)
+        kwg = [lap.tile([P, KCH], U32, name="kwg0", offset=0, align_bytes=64), sb.tile([P, KCH], U32, name="kwg1", tag="late", align_bytes=64)]
+        a_ps = []
+        for h in range(I // KCH):
+            gather(kwg[h], kw, h * KCH, KCH)
+            a = ps.tile([P, KCH], F32, name="a%d" % h)
+            mx(a[:], q_c[:], q_s[:], kwg[h][:], ksg[:, h * KCH:(h + 1) * KCH])
+            a_ps.append(a)
+        acc = sb.tile([P, T], F32, name="acc", tag="pool_a")
+        nc.sync.dma_start(out=acc[:], in_=old)
+
+        gk = KCH // PAGE
+        nm = sb.tile([P, G], F32, name="nm")
+        for h in range(I // KCH):
+            if PER_PAGE[h]:
+                nc.vector.tensor_reduce(out=nm[:, h * gk:(h + 1) * gk], in_=a_ps[h][:].rearrange("p (g j) -> p g j", j=PAGE), axis=AX.X, op=ALU.max, negate=True)
+            else:
+                nc.vector.tensor_reduce(out=nm[:, h * gk:h * gk + 1], in_=a_ps[h][:], axis=AX.X, op=ALU.max, negate=True)
+
+        two_c, two_s = quant(two_g[:], "two")
+        pg_c, pg_s = quant(pg_g[:], "pg")
+        b_ps = ps.tile([P, U], F32, name="b")
+        mx(b_ps[:], two_c[:, 0:Q], two_s[:, 0:Q], pg_c[:], pg_s[:])
+        nmb = sb.tile([P, 1], F32, name="nmb")
+        nc.vector.tensor_reduce(out=nmb[:], in_=b_ps[:], axis=AX.X, op=ALU.max, negate=True)
+        pb = sb.tile([P, U], F32, name="pb")
+        sb_sum = sb.tile([P, 1], F32, name="sb_sum")
+        nc.scalar.activation(out=pb[:], in_=b_ps[:], func=ACT.Exp, bias=nmb[:], accum_out=sb_sum[:])
+        rb = sb.tile([P, 1], F32, name="rb")
+        nc.vector.reciprocal(out=rb[:], in_=sb_sum[:])
+        mb = sb.tile([P, U], F32, name="mb")
+        nc.scalar.activation(out=mb[:], in_=pb[:], func=ACT.Copy, scale=rb[:])
+        mg = sb.tile([P, G], F32, name="mg")
+        nc.vector.tensor_copy(out=mg[:], in_=mb[:].indirect(offs2_t[:]))
+
+        pa = sb.tile([P, I], F32, name="pa")
+        s0 = sb.tile([P, G], F32, name="s0")
+        zi = sb.tile([P, G], F32, name="zi")
+        cf = sb.tile([P, G], F32, name="cf")
+        kf = sb.tile([P, G], F32, name="kf")
+        for h in range(I // KCH):
+            gs = slice(h * gk, (h + 1) * gk)
+            if PER_PAGE[h]:
+                for g in range(gk):
+                    gg = h * gk + g
+                    nc.scalar.activation(out=pa[:, gg * PAGE:(gg + 1) * PAGE], in_=a_ps[h][:, g * PAGE:(g + 1) * PAGE], func=ACT.Exp, bias=nm[:, gg:gg + 1], accum_out=s0[:, gg:gg + 1])
+            else:
+                nc.scalar.activation(out=pa[:, h * KCH:(h + 1) * KCH], in_=a_ps[h][:], func=ACT.Exp, bias=nm[:, h * gk:h * gk + 1])
+                nc.vector.tensor_reduce(out=s0[:, gs], in_=pa[:, h * KCH:(h + 1) * KCH].rearrange("p (g j) -> p g j", j=PAGE), axis=AX.X, op=ALU.add)
+        nc.vector.reciprocal(out=zi[:], in_=s0[:])
+        nc.vector.scalar_tensor_tensor(out=cf[:], in0=zi[:], scalar=256.0, in1=mg[:], op0=ALU.mult, op1=ALU.mult)
+        nc.vector.scalar_tensor_tensor(out=kf[:], in0=cf[:], scalar=-1.0, in1=zi[:], op0=ALU.mult, op1=ALU.mult)
+
+        vsg = sb.tile([P, I], U8, name="vsg", tag="late", align_bytes=64)
+        gather(vsg, vs, 0, I)
+        dp_ps = []
+        for k in range(I // VCH):
+            vwg = sb.tile([P, VCH], U32, name="vwg%d" % k, align_bytes=64)
+            gather(vwg, vw, k * VCH, VCH)
+            dp = ps.tile([P, VCH], F32, name="dp%d" % k)
+            mx(dp[:], two_c[:, Q:], two_s[:, Q:], vwg[:], vsg[:, k * VCH:(k + 1) * VCH])
+            dp_ps.append(dp)
+
+        gv = VCH // PAGE
+        s1 = sb.tile([P, G], F32, name="s1")
+        nb = sb.tile([P, G], F32, name="nb")
+        ws = []
+        for k in range(I // VCH):
+            cs = slice(k * VCH, (k + 1) * VCH)
+            gs = slice(k * gv, (k + 1) * gv)
+            e = sb.tile([P, VCH], F32, name="e%d" % k)
+            nc.vector.tensor_tensor(out=e[:], in0=dp_ps[k][:], in1=pa[:, cs], op=ALU.mult)
+            nc.vector.tensor_reduce(out=s1[:, gs], in_=e[:].rearrange("p (g j) -> p g j", j=PAGE), axis=AX.X, op=ALU.add)
+            nc.vector.tensor_tensor(out=nb[:, gs], in0=s1[:, gs], in1=kf[:, gs], op=ALU.mult)
+            w = sb.tile([P, VCH], F32, name="w%d" % k)
+            for g in range(gv):
+                gg = k * gv + g
+                nc.scalar.activation(out=w[:, g * PAGE:(g + 1) * PAGE], in_=dp_ps[k][:, g * PAGE:(g + 1) * PAGE], func=ACT.Identity, scale=cf[:, gg:gg + 1], bias=nb[:, gg:gg + 1])
+            ws.append(w)
+        for k in range(I // VCH):
+            nc.vector.tensor_tensor(out=df[:].indirect(offs_t[:, k * VCH // 16:(k + 1) * VCH // 16]), in0=pa[:, k * VCH:(k + 1) * VCH], in1=ws[k][:], op=ALU.mult)
+
+        lo = 0
+        for c, width in enumerate((256, 512, 512, 384, 256, 128)):
+            cs = slice(lo, lo + width)
+            lo = lo + width
+            nc.vector.tensor_tensor(out=acc[:, cs], in0=acc[:, cs], in1=df[:, cs], op=ALU.add)
+            (nc.sync if c % 2 == 0 else nc.scalar).dma_start(out=out[:, cs], in_=acc[:, cs])

@@ -1,6 +1,7 @@
 from contextlib import ExitStack
 
 import concourse.mybir as mybir
+from concourse.masks import make_identity
 
 D, E, T, I, G, U, Q = 512, 512, 2048, 1024, 64, 256, 128
 FLOPS = 2 * Q * (D * U + D * I + E * I)
@@ -20,8 +21,7 @@ P = 128
 PACK = 4
 PAGE = I // G
 KCH = 512
-VCH = 256
-PER_PAGE = (False, False)
+VCHUNKS = (256, 256, 256, 256)
 
 
 def tile_attend_gwithinpage_kernel(tc, query, keys_words, keys_scales, pquery, pgsum, gout, vals_words, vals_scales, old, offs, offs2, out):
@@ -43,10 +43,10 @@ def tile_attend_gwithinpage_kernel(tc, query, keys_words, keys_scales, pquery, p
         def load_words(src, t):
             nc.sync.dma_start(out=t[:].bitcast(I32), in_=src[0].rearrange("p n t -> p (n t)").bitcast(I32))
 
-        def load_scales(src, t, queue):
+        def load_scales(src, t):
             nc.vector.memset(t[:].bitcast(I32), 0)
             for r in range(4):
-                queue.dma_start(out=t[r:P:32, :].bitcast(I32), in_=src[0, r:16:4, :].bitcast(I32))
+                nc.sync.dma_start(out=t[r:P:32, :].bitcast(I32), in_=src[0, r:16:4, :].bitcast(I32))
 
         def cast(raw, g):
             nc.scalar.activation(out=g.rearrange("p (c i t) -> p c t i", i=4, t=PACK), in_=raw.rearrange("p t (c i) -> p c t i", i=4), func=ACT.Copy)
@@ -65,59 +65,75 @@ def tile_attend_gwithinpage_kernel(tc, query, keys_words, keys_scales, pquery, p
             nc.tensor.matmul_mx(out=acc, lhsT=lc.bitcast(FP8X4), lhsT_scale=ls, rhs=rc.bitcast(FP8X4), rhs_scale=rs, start=True, stop=True)
 
         nc.sync.dma_start(offs_t[:], offs)
-        raw0 = sb.tile([P, PACK * Q], F32, name="raw0", tag="raw")
-        q_raw = load_raw(query, raw0[:])
+        raw0 = lap.tile([P, 1408], F32, name="raw0", offset=7168)
+        q_raw = load_raw(query, raw0[:, 0:PACK * Q])
         nc.sync.dma_start(offs2_t[:], offs2)
-        kw = sb.tile([P, T], U32, name="kw", tag="pool_a")
-        load_words(keys_words, kw)
-        ks = lap.tile([P, T], U8, name="ks", offset=1024)
-        load_scales(keys_scales, ks, nc.scalar)
+        ks = sb.tile([P, T], U8, name="ks", tag="kv")
+        load_scales(keys_scales, ks)
         vs = sb.tile([P, T], U8, name="vs")
-        load_scales(vals_scales, vs, nc.gpsimd)
+        load_scales(vals_scales, vs)
         df = sb.tile([P, T], F32, name="df")
         nc.vector.memset(df[:], 0.0)
+        ident = sb.tile([P, P], F32, name="ident")
+        make_identity(nc, ident[:])
 
-        q_g = sb.tile([P, Q * PACK], BF16, name="q_g", tag="pool_b", align_bytes=64)
-        nc.vector.tensor_copy(out=q_g[:].rearrange("p (c i t) -> p c t i", i=4, t=PACK), in_=q_raw.rearrange("p t (c i) -> p c t i", i=4))
-        q_c, q_s = quant(q_g[:], "q")
-        raw1 = sb.tile([P, PACK * 2 * Q], F32, name="raw1", tag="raw")
-        pq_raw = load_raw(pquery, raw1[:, 0:PACK * Q])
-        go_raw = load_raw(gout, raw1[:, PACK * Q:])
-        raw2 = sb.tile([P, PACK * U], F32, name="raw2", tag="pool_b", align_bytes=64)
-        pg_raw = load_raw(pgsum, raw2[:])
-
-        two_g = sb.tile([P, PACK * 2 * Q], BF16, name="two_g", align_bytes=64)
-        pg_g = sb.tile([P, PACK * U], BF16, name="pg_g", align_bytes=64)
-        cast(pq_raw, two_g[:, 0:PACK * Q])
-        cast(go_raw, two_g[:, PACK * Q:])
-        cast(pg_raw, pg_g[:])
+        q_g = sb.tile([P, Q * PACK], BF16, name="q_g", align_bytes=64)
+        cast(q_raw, q_g[:])
+        kw = lap.tile([P, T], U32, name="kw", offset=0)
+        load_words(keys_words, kw)
+        raw_pg = lap.tile([P, PACK * U], F32, name="raw_pg", offset=12288)
+        pg_raw = load_raw(pgsum, raw_pg[:])
+        raw_pq = lap.tile([P, PACK * Q], F32, name="raw_pq", offset=10240)
+        pq_raw = load_raw(pquery, raw_pq[:])
+        raw_go = lap.tile([P, PACK * Q], F32, name="raw_go", offset=8192)
+        go_raw = load_raw(gout, raw_go[:])
 
         ksg = sb.tile([P, I], U8, name="ksg", align_bytes=64)
         gather(ksg, ks, 0, I)
-        vw = lap.tile([P, T], U32, name="vw", offset=2048)
+        vw = sb.tile([P, T], U32, name="vw", tag="kv")
         load_words(vals_words, vw)
-        kwg = [lap.tile([P, KCH], U32, name="kwg0", offset=0, align_bytes=64), sb.tile([P, KCH], U32, name="kwg1", tag="late", align_bytes=64)]
+        q_c, q_s = quant(q_g[:], "q")
+        vsg = sb.tile([P, I], U8, name="vsg", align_bytes=64)
+        gather(vsg, vs, 0, I)
+
+        two_g = sb.tile([P, PACK * 2 * Q], BF16, name="two_g", align_bytes=64)
+        pg_g = sb.tile([P, PACK * U], BF16, name="pg_g", align_bytes=64)
+        cast(pg_raw, pg_g[:])
+        cast(pq_raw, two_g[:, 0:PACK * Q])
+
         a_ps = []
         for h in range(I // KCH):
-            gather(kwg[h], kw, h * KCH, KCH)
-            a = ps.tile([P, KCH], F32, name="a%d" % h)
-            mx(a[:], q_c[:], q_s[:], kwg[h][:], ksg[:, h * KCH:(h + 1) * KCH])
+            kwg = sb.tile([P, KCH], U32, name="kwg%d" % h, align_bytes=64)
+            gather(kwg, kw, h * KCH, KCH)
+            a = ps.tile([P, KCH], F32, name="a%d" % h, tag="a%d" % h)
+            mx(a[:], q_c[:], q_s[:], kwg[:], ksg[:, h * KCH:(h + 1) * KCH])
             a_ps.append(a)
-        acc = sb.tile([P, T], F32, name="acc", tag="pool_a")
+        acc = lap.tile([P, T], F32, name="acc", offset=0)
         nc.sync.dma_start(out=acc[:], in_=old)
 
         gk = KCH // PAGE
-        nm = sb.tile([P, G], F32, name="nm")
+        nm = sb.tile([P, I // KCH], F32, name="nm")
         for h in range(I // KCH):
-            if PER_PAGE[h]:
-                nc.vector.tensor_reduce(out=nm[:, h * gk:(h + 1) * gk], in_=a_ps[h][:].rearrange("p (g j) -> p g j", j=PAGE), axis=AX.X, op=ALU.max, negate=True)
-            else:
-                nc.vector.tensor_reduce(out=nm[:, h * gk:h * gk + 1], in_=a_ps[h][:], axis=AX.X, op=ALU.max, negate=True)
+            nc.vector.tensor_reduce(out=nm[:, h:h + 1], in_=a_ps[h][:], axis=AX.X, op=ALU.max, negate=True)
 
-        two_c, two_s = quant(two_g[:], "two")
+        pa = sb.tile([P, I], F32, name="pa")
+        runs = I // P
+        dealt = sb.tile([P, runs, P], F32, name="dealt")
+        for h in range(I // KCH):
+            nc.scalar.activation(out=dealt[:, :, h * KCH // runs:(h + 1) * KCH // runs], in_=a_ps[h][:].rearrange("p (m r) -> p r m", r=runs), func=ACT.Exp, bias=nm[:, h:h + 1])
+        cast(go_raw, two_g[:, PACK * Q:])
+        turned = ps.tile([P, P], F32, name="turned", tag="turned")
+        for j in range(runs):
+            nc.tensor.matmul(turned[:], lhsT=dealt[:, j, :], rhs=ident[:], is_transpose=True, start=(j == 0), stop=(j == runs - 1))
+        halves_t = sb.tile([P, P], F32, name="halves_t")
+        nc.scalar.copy(out=halves_t[:], in_=turned[:])
+        halves = ps.tile([P, P], F32, name="halves", tag="x")
+        nc.tensor.transpose(halves[:], halves_t[:], ident[:])
         pg_c, pg_s = quant(pg_g[:], "pg")
+        pq_c, pq_s = quant(two_g[:, 0:PACK * Q], "pq")
+        go_c, go_s = quant(two_g[:, PACK * Q:], "go")
         b_ps = ps.tile([P, U], F32, name="b")
-        mx(b_ps[:], two_c[:, 0:Q], two_s[:, 0:Q], pg_c[:], pg_s[:])
+        mx(b_ps[:], pq_c[:], pq_s[:], pg_c[:], pg_s[:])
         nmb = sb.tile([P, 1], F32, name="nmb")
         nc.vector.tensor_reduce(out=nmb[:], in_=b_ps[:], axis=AX.X, op=ALU.max, negate=True)
         pb = sb.tile([P, U], F32, name="pb")
@@ -130,55 +146,47 @@ def tile_attend_gwithinpage_kernel(tc, query, keys_words, keys_scales, pquery, p
         mg = sb.tile([P, G], F32, name="mg")
         nc.vector.tensor_copy(out=mg[:], in_=mb[:].indirect(offs2_t[:]))
 
-        pa = sb.tile([P, I], F32, name="pa")
-        s0 = sb.tile([P, G], F32, name="s0")
+        s0 = sb.tile([P, G], F32, name="s0", tag="late")
         zi = sb.tile([P, G], F32, name="zi")
         cf = sb.tile([P, G], F32, name="cf")
         kf = sb.tile([P, G], F32, name="kf")
         for h in range(I // KCH):
-            gs = slice(h * gk, (h + 1) * gk)
-            if PER_PAGE[h]:
-                for g in range(gk):
-                    gg = h * gk + g
-                    nc.scalar.activation(out=pa[:, gg * PAGE:(gg + 1) * PAGE], in_=a_ps[h][:, g * PAGE:(g + 1) * PAGE], func=ACT.Exp, bias=nm[:, gg:gg + 1], accum_out=s0[:, gg:gg + 1])
-            else:
-                nc.scalar.activation(out=pa[:, h * KCH:(h + 1) * KCH], in_=a_ps[h][:], func=ACT.Exp, bias=nm[:, h * gk:h * gk + 1])
-                nc.vector.tensor_reduce(out=s0[:, gs], in_=pa[:, h * KCH:(h + 1) * KCH].rearrange("p (g j) -> p g j", j=PAGE), axis=AX.X, op=ALU.add)
+            nc.scalar.activation(out=pa[:, h * KCH:(h + 1) * KCH], in_=a_ps[h][:], func=ACT.Exp, bias=nm[:, h:h + 1])
+        nc.vector.tensor_reduce(out=s0[:], in_=halves[:].rearrange("p (g j) -> p g j", j=PAGE // runs), axis=AX.X, op=ALU.add)
         nc.vector.reciprocal(out=zi[:], in_=s0[:])
         nc.vector.scalar_tensor_tensor(out=cf[:], in0=zi[:], scalar=256.0, in1=mg[:], op0=ALU.mult, op1=ALU.mult)
         nc.vector.scalar_tensor_tensor(out=kf[:], in0=cf[:], scalar=-1.0, in1=zi[:], op0=ALU.mult, op1=ALU.mult)
 
-        vsg = sb.tile([P, I], U8, name="vsg", tag="late", align_bytes=64)
-        gather(vsg, vs, 0, I)
+        starts = [sum(VCHUNKS[:k]) for k in range(len(VCHUNKS))]
         dp_ps = []
-        for k in range(I // VCH):
-            vwg = sb.tile([P, VCH], U32, name="vwg%d" % k, align_bytes=64)
-            gather(vwg, vw, k * VCH, VCH)
-            dp = ps.tile([P, VCH], F32, name="dp%d" % k)
-            mx(dp[:], two_c[:, Q:], two_s[:, Q:], vwg[:], vsg[:, k * VCH:(k + 1) * VCH])
+        for k, (lo, n) in enumerate(zip(starts, VCHUNKS)):
+            vwg = sb.tile([P, n], U32, name="vwg%d" % k, align_bytes=64)
+            gather(vwg, vw, lo, n)
+            dp = ps.tile([P, n], F32, name="dp%d" % k, tag=("dp0", "dp1", "dp2", "turned")[k])
+            mx(dp[:], go_c[:], go_s[:], vwg[:], vsg[:, lo:lo + n])
             dp_ps.append(dp)
 
-        gv = VCH // PAGE
         s1 = sb.tile([P, G], F32, name="s1")
         nb = sb.tile([P, G], F32, name="nb")
         ws = []
-        for k in range(I // VCH):
-            cs = slice(k * VCH, (k + 1) * VCH)
-            gs = slice(k * gv, (k + 1) * gv)
-            e = sb.tile([P, VCH], F32, name="e%d" % k)
-            nc.vector.tensor_tensor(out=e[:], in0=dp_ps[k][:], in1=pa[:, cs], op=ALU.mult)
-            nc.vector.tensor_reduce(out=s1[:, gs], in_=e[:].rearrange("p (g j) -> p g j", j=PAGE), axis=AX.X, op=ALU.add)
+        e_first = sb.tile([P, VCHUNKS[0]], F32, name="e_first")
+        e_rest = sb.tile([P, I - VCHUNKS[0]], F32, name="e_rest", tag="late")
+        for k, (lo, n) in enumerate(zip(starts, VCHUNKS)):
+            gs = slice(lo // PAGE, (lo + n) // PAGE)
+            e = e_first[:] if k == 0 else e_rest[:, lo - VCHUNKS[0]:lo - VCHUNKS[0] + n]
+            nc.vector.tensor_tensor(out=e, in0=dp_ps[k][:], in1=pa[:, lo:lo + n], op=ALU.mult)
+            nc.vector.tensor_reduce(out=s1[:, gs], in_=e.rearrange("p (g j) -> p g j", j=PAGE), axis=AX.X, op=ALU.add)
             nc.vector.tensor_tensor(out=nb[:, gs], in0=s1[:, gs], in1=kf[:, gs], op=ALU.mult)
-            w = sb.tile([P, VCH], F32, name="w%d" % k)
-            for g in range(gv):
-                gg = k * gv + g
+            w = sb.tile([P, n], F32, name="w%d" % k)
+            for g in range(n // PAGE):
+                gg = lo // PAGE + g
                 nc.scalar.activation(out=w[:, g * PAGE:(g + 1) * PAGE], in_=dp_ps[k][:, g * PAGE:(g + 1) * PAGE], func=ACT.Identity, scale=cf[:, gg:gg + 1], bias=nb[:, gg:gg + 1])
             ws.append(w)
-        for k in range(I // VCH):
-            nc.vector.tensor_tensor(out=df[:].indirect(offs_t[:, k * VCH // 16:(k + 1) * VCH // 16]), in0=pa[:, k * VCH:(k + 1) * VCH], in1=ws[k][:], op=ALU.mult)
+        for k, (lo, n) in enumerate(zip(starts, VCHUNKS)):
+            nc.vector.tensor_tensor(out=df[:].indirect(offs_t[:, lo // 16:(lo + n) // 16]), in0=pa[:, lo:lo + n], in1=ws[k][:], op=ALU.mult)
 
         lo = 0
-        for c, width in enumerate((256, 512, 512, 384, 256, 128)):
+        for c, width in enumerate((384, 512, 640, 512)):
             cs = slice(lo, lo + width)
             lo = lo + width
             nc.vector.tensor_tensor(out=acc[:, cs], in0=acc[:, cs], in1=df[:, cs], op=ALU.add)

@@ -21,7 +21,7 @@ P = 128
 PACK = 4
 PAGE = I // G
 KCH = 512
-VCHUNKS = (256, 256, 256, 256)
+VCHUNKS = (256, 256, 512)
 
 
 def tile_attend_gwithinpage_kernel(tc, query, keys_words, keys_scales, pquery, pgsum, gout, vals_words, vals_scales, old, offs, offs2, out):
@@ -77,6 +77,8 @@ def tile_attend_gwithinpage_kernel(tc, query, keys_words, keys_scales, pquery, p
         ident = sb.tile([P, P], F32, name="ident")
         make_identity(nc, ident[:])
 
+        gain = sb.tile([P, G], F32, name="gain")
+        nc.gpsimd.memset(gain[:], 256.0)
         q_g = sb.tile([P, Q * PACK], BF16, name="q_g", align_bytes=64)
         cast(q_raw, q_g[:])
         kw = lap.tile([P, T], U32, name="kw", offset=0)
@@ -144,7 +146,7 @@ def tile_attend_gwithinpage_kernel(tc, query, keys_words, keys_scales, pquery, p
         mb = sb.tile([P, U], F32, name="mb")
         nc.scalar.activation(out=mb[:], in_=pb[:], func=ACT.Copy, scale=rb[:])
         mg = sb.tile([P, G], F32, name="mg")
-        nc.vector.tensor_copy(out=mg[:], in_=mb[:].indirect(offs2_t[:]))
+        nc.vector.tensor_tensor(out=mg[:], in0=mb[:].indirect(offs2_t[:]), in1=gain[:], op=ALU.mult)
 
         s0 = sb.tile([P, G], F32, name="s0", tag="late")
         zi = sb.tile([P, G], F32, name="zi")
@@ -154,15 +156,15 @@ def tile_attend_gwithinpage_kernel(tc, query, keys_words, keys_scales, pquery, p
             nc.scalar.activation(out=pa[:, h * KCH:(h + 1) * KCH], in_=a_ps[h][:], func=ACT.Exp, bias=nm[:, h:h + 1])
         nc.vector.tensor_reduce(out=s0[:], in_=halves[:].rearrange("p (g j) -> p g j", j=PAGE // runs), axis=AX.X, op=ALU.add)
         nc.vector.reciprocal(out=zi[:], in_=s0[:])
-        nc.vector.scalar_tensor_tensor(out=cf[:], in0=zi[:], scalar=256.0, in1=mg[:], op0=ALU.mult, op1=ALU.mult)
-        nc.vector.scalar_tensor_tensor(out=kf[:], in0=cf[:], scalar=-1.0, in1=zi[:], op0=ALU.mult, op1=ALU.mult)
+        nc.gpsimd.tensor_tensor(out=cf[:], in0=zi[:], in1=mg[:], op=ALU.mult)
+        nc.gpsimd.tensor_tensor(out=kf[:], in0=cf[:], in1=zi[:], op=ALU.mult)
 
         starts = [sum(VCHUNKS[:k]) for k in range(len(VCHUNKS))]
         dp_ps = []
         for k, (lo, n) in enumerate(zip(starts, VCHUNKS)):
             vwg = sb.tile([P, n], U32, name="vwg%d" % k, align_bytes=64)
             gather(vwg, vw, lo, n)
-            dp = ps.tile([P, n], F32, name="dp%d" % k, tag=("dp0", "dp1", "dp2", "turned")[k])
+            dp = ps.tile([P, n], F32, name="dp%d" % k, tag="x" if k == len(VCHUNKS) - 1 else "dp%d" % k)
             mx(dp[:], go_c[:], go_s[:], vwg[:], vsg[:, lo:lo + n])
             dp_ps.append(dp)
 
@@ -175,8 +177,8 @@ def tile_attend_gwithinpage_kernel(tc, query, keys_words, keys_scales, pquery, p
             gs = slice(lo // PAGE, (lo + n) // PAGE)
             e = e_first[:] if k == 0 else e_rest[:, lo - VCHUNKS[0]:lo - VCHUNKS[0] + n]
             nc.vector.tensor_tensor(out=e, in0=dp_ps[k][:], in1=pa[:, lo:lo + n], op=ALU.mult)
-            nc.vector.tensor_reduce(out=s1[:, gs], in_=e.rearrange("p (g j) -> p g j", j=PAGE), axis=AX.X, op=ALU.add)
-            nc.vector.tensor_tensor(out=nb[:, gs], in0=s1[:, gs], in1=kf[:, gs], op=ALU.mult)
+            nc.vector.tensor_reduce(out=s1[:, gs], in_=e.rearrange("p (g j) -> p g j", j=PAGE), axis=AX.X, op=ALU.add, negate=True)
+            nc.gpsimd.tensor_tensor(out=nb[:, gs], in0=s1[:, gs], in1=kf[:, gs], op=ALU.mult)
             w = sb.tile([P, n], F32, name="w%d" % k)
             for g in range(n // PAGE):
                 gg = lo // PAGE + g
@@ -186,7 +188,7 @@ def tile_attend_gwithinpage_kernel(tc, query, keys_words, keys_scales, pquery, p
             nc.vector.tensor_tensor(out=df[:].indirect(offs_t[:, lo // 16:(lo + n) // 16]), in0=pa[:, lo:lo + n], in1=ws[k][:], op=ALU.mult)
 
         lo = 0
-        for c, width in enumerate((384, 512, 640, 512)):
+        for c, width in enumerate((256, 512, 640, 640)):
             cs = slice(lo, lo + width)
             lo = lo + width
             nc.vector.tensor_tensor(out=acc[:, cs], in0=acc[:, cs], in1=df[:, cs], op=ALU.add)

@@ -20,8 +20,20 @@ AX = mybir.AxisListType
 P = 128
 PACK = 4
 PAGE = I // G
-KCH = 512
-VCHUNKS = (256, 256, 512)
+PER_COLUMN = 16
+HALF = 512
+RUN = I // P
+
+CHUNKS = (256, 256, 512)
+STORES = (256, 512, 640, 640)
+
+AT_PA = 1024
+AT_QUERY = 4096
+QUERY_STAGE = 1280
+AT_GOUT = 4096
+AT_DEALT = 5120
+AT_PQUERY = 6144
+AT_PGSUM = 8192
 
 
 def tile_attend_gwithinpage_kernel(tc, query, keys_words, keys_scales, pquery, pgsum, gout, vals_words, vals_scales, old, offs, offs2, out):
@@ -29,167 +41,171 @@ def tile_attend_gwithinpage_kernel(tc, query, keys_words, keys_scales, pquery, p
     with ExitStack() as ctx:
         lists = ctx.enter_context(tc.tile_pool(name="lists", bufs=1))
         sb = ctx.enter_context(tc.tile_pool(name="sb", bufs=1))
-        lap = ctx.enter_context(tc.tile_pool(name="lap", bufs=1))
+        shared = ctx.enter_context(tc.tile_pool(name="shared", bufs=1))
         ps = ctx.enter_context(tc.psum_pool(name="ps", bufs=1))
 
-        offs_t = lists.tile([P, I // 16], U16, name="offs_t")
-        offs2_t = lists.tile([P, G // 16], U16, name="offs2_t")
+        offs_t = lists.tile([P, I // PER_COLUMN], U16, name="offs_t")
+        offs2_t = lists.tile([P, G // PER_COLUMN], U16, name="offs2_t")
 
-        def load_raw(src, flat):
-            raw = flat.rearrange("p (j w) -> p j w", j=PACK)
-            nc.sync.dma_start(out=raw, in_=src.rearrange("(p j) w -> p j w", j=PACK))
-            return raw
+        def slots(lo, n):
+            return offs_t[:, lo // PER_COLUMN:(lo + n) // PER_COLUMN]
 
-        def load_words(src, t):
-            nc.sync.dma_start(out=t[:].bitcast(I32), in_=src[0].rearrange("p n t -> p (n t)").bitcast(I32))
+        def load_rows(src, flat):
+            rows = flat.rearrange("p (t w) -> p t w", t=PACK)
+            nc.sync.dma_start(out=rows, in_=src.rearrange("(p t) w -> p t w", t=PACK))
+            return rows
 
-        def load_scales(src, t):
-            nc.vector.memset(t[:].bitcast(I32), 0)
+        def load_words(src, window):
+            nc.sync.dma_start(out=window[:].bitcast(I32), in_=src[0].rearrange("p n t -> p (n t)").bitcast(I32))
+
+        def load_scales(src, window):
+            nc.vector.memset(window[:, 0:T // 2].bitcast(I32), 0)
+            nc.gpsimd.memset(window[:, T // 2:].bitcast(I32), 0)
             for r in range(4):
-                nc.sync.dma_start(out=t[r:P:32, :].bitcast(I32), in_=src[0, r:16:4, :].bitcast(I32))
+                nc.sync.dma_start(out=window[r:P:32, :].bitcast(I32), in_=src[0, r:16:4, :].bitcast(I32))
 
-        def cast(raw, g):
-            nc.scalar.activation(out=g.rearrange("p (c i t) -> p c t i", i=4, t=PACK), in_=raw.rearrange("p t (c i) -> p c t i", i=4), func=ACT.Copy)
+        def interleave(rows, grouped):
+            nc.scalar.activation(out=grouped.rearrange("p (c i t) -> p c t i", i=4, t=PACK), in_=rows.rearrange("p t (c i) -> p c t i", i=4), func=ACT.Copy)
 
-        def quant(g, name):
-            width = g.shape[1] // PACK
-            codes = sb.tile([P, width], U32, name=name + "_c", align_bytes=64)
-            scales = sb.tile([P, width], U8, name=name + "_s", align_bytes=64)
-            nc.vector.quantize_mx(out=codes[:].bitcast(FP8X4), scales=scales[:], in_=g)
+        def quantize(grouped, name):
+            width = grouped.shape[1] // PACK
+            codes = sb.tile([P, width], U32, name=name + "_codes", align_bytes=64)
+            scales = sb.tile([P, width], U8, name=name + "_scales", align_bytes=64)
+            nc.vector.quantize_mx(out=codes[:].bitcast(FP8X4), scales=scales[:], in_=grouped)
             return codes, scales
 
-        def gather(t, window, lo, n):
-            nc.vector.tensor_copy(out=t[:], in_=window[:].indirect(offs_t[:, lo // 16:(lo + n) // 16]))
+        def gather(dst, window, lo, n):
+            nc.vector.tensor_copy(out=dst[:], in_=window[:].indirect(slots(lo, n)))
 
-        def mx(acc, lc, ls, rc, rs):
-            nc.tensor.matmul_mx(out=acc, lhsT=lc.bitcast(FP8X4), lhsT_scale=ls, rhs=rc.bitcast(FP8X4), rhs_scale=rs, start=True, stop=True)
+        def product(acc, lhs_codes, lhs_scales, rhs_codes, rhs_scales):
+            nc.tensor.matmul_mx(out=acc, lhsT=lhs_codes.bitcast(FP8X4), lhsT_scale=lhs_scales, rhs=rhs_codes.bitcast(FP8X4), rhs_scale=rhs_scales, start=True, stop=True)
 
         nc.sync.dma_start(offs_t[:], offs)
-        raw0 = lap.tile([P, 1408], F32, name="raw0", offset=7168)
-        q_raw = load_raw(query, raw0[:, 0:PACK * Q])
         nc.sync.dma_start(offs2_t[:], offs2)
-        ks = sb.tile([P, T], U8, name="ks", tag="kv")
-        load_scales(keys_scales, ks)
-        vs = sb.tile([P, T], U8, name="vs")
-        load_scales(vals_scales, vs)
+        query_stage = shared.tile([P, QUERY_STAGE], F32, name="query_stage", offset=AT_QUERY)
+        query_rows = load_rows(query, query_stage[:, 0:PACK * Q])
+        key_scales = sb.tile([P, T], U8, name="key_scales", tag="key_scales_then_val_words")
+        load_scales(keys_scales, key_scales)
+        key_words = sb.tile([P, T], U32, name="key_words", tag="key_words_then_old")
+        load_words(keys_words, key_words)
+        val_scales = sb.tile([P, T], U8, name="val_scales")
+        load_scales(vals_scales, val_scales)
         df = sb.tile([P, T], F32, name="df")
         nc.vector.memset(df[:], 0.0)
         ident = sb.tile([P, P], F32, name="ident")
         make_identity(nc, ident[:])
-
         gain = sb.tile([P, G], F32, name="gain")
         nc.gpsimd.memset(gain[:], 256.0)
-        q_g = sb.tile([P, Q * PACK], BF16, name="q_g", align_bytes=64)
-        cast(q_raw, q_g[:])
-        kw = lap.tile([P, T], U32, name="kw", offset=0)
-        load_words(keys_words, kw)
-        raw_pg = lap.tile([P, PACK * U], F32, name="raw_pg", offset=12288)
-        pg_raw = load_raw(pgsum, raw_pg[:])
-        raw_pq = lap.tile([P, PACK * Q], F32, name="raw_pq", offset=10240)
-        pq_raw = load_raw(pquery, raw_pq[:])
-        raw_go = lap.tile([P, PACK * Q], F32, name="raw_go", offset=8192)
-        go_raw = load_raw(gout, raw_go[:])
 
-        ksg = sb.tile([P, I], U8, name="ksg", align_bytes=64)
-        gather(ksg, ks, 0, I)
-        vw = sb.tile([P, T], U32, name="vw", tag="kv")
-        load_words(vals_words, vw)
-        q_c, q_s = quant(q_g[:], "q")
-        vsg = sb.tile([P, I], U8, name="vsg", align_bytes=64)
-        gather(vsg, vs, 0, I)
+        query_bf = sb.tile([P, PACK * Q], BF16, name="query_bf", align_bytes=64)
+        interleave(query_rows, query_bf[:])
+        pgsum_stage = shared.tile([P, PACK * U], F32, name="pgsum_stage", offset=AT_PGSUM)
+        pgsum_rows = load_rows(pgsum, pgsum_stage[:])
+        pquery_stage = shared.tile([P, PACK * Q], F32, name="pquery_stage", offset=AT_PQUERY)
+        pquery_rows = load_rows(pquery, pquery_stage[:])
+        gout_stage = shared.tile([P, PACK * Q], F32, name="gout_stage", offset=AT_GOUT)
+        gout_rows = load_rows(gout, gout_stage[:])
 
-        two_g = sb.tile([P, PACK * 2 * Q], BF16, name="two_g", align_bytes=64)
-        pg_g = sb.tile([P, PACK * U], BF16, name="pg_g", align_bytes=64)
-        cast(pg_raw, pg_g[:])
-        cast(pq_raw, two_g[:, 0:PACK * Q])
+        listed_key_scales = sb.tile([P, I], U8, name="listed_key_scales", align_bytes=64)
+        gather(listed_key_scales, key_scales, 0, I)
+        val_words = sb.tile([P, T], U32, name="val_words", tag="key_scales_then_val_words")
+        load_words(vals_words, val_words)
+        query_codes, query_scales = quantize(query_bf[:], "query")
 
-        a_ps = []
-        for h in range(I // KCH):
-            kwg = sb.tile([P, KCH], U32, name="kwg%d" % h, align_bytes=64)
-            gather(kwg, kw, h * KCH, KCH)
-            a = ps.tile([P, KCH], F32, name="a%d" % h, tag="a%d" % h)
-            mx(a[:], q_c[:], q_s[:], kwg[:], ksg[:, h * KCH:(h + 1) * KCH])
-            a_ps.append(a)
-        acc = lap.tile([P, T], F32, name="acc", offset=0)
-        nc.sync.dma_start(out=acc[:], in_=old)
+        pair_bf = sb.tile([P, PACK * 2 * Q], BF16, name="pair_bf", align_bytes=64)
+        pgsum_bf = sb.tile([P, PACK * U], BF16, name="pgsum_bf", align_bytes=64)
+        interleave(pgsum_rows, pgsum_bf[:])
+        interleave(pquery_rows, pair_bf[:, 0:PACK * Q])
+        interleave(gout_rows, pair_bf[:, PACK * Q:])
 
-        gk = KCH // PAGE
-        nm = sb.tile([P, I // KCH], F32, name="nm")
-        for h in range(I // KCH):
-            nc.vector.tensor_reduce(out=nm[:, h:h + 1], in_=a_ps[h][:], axis=AX.X, op=ALU.max, negate=True)
+        scores = []
+        for h in range(I // HALF):
+            listed_key_words = sb.tile([P, HALF], U32, name="listed_key_words%d" % h, tag="listed%d" % h, align_bytes=64)
+            gather(listed_key_words, key_words, h * HALF, HALF)
+            a = ps.tile([P, HALF], F32, name="a%d" % h)
+            product(a[:], query_codes[:], query_scales[:], listed_key_words[:], listed_key_scales[:, h * HALF:(h + 1) * HALF])
+            scores.append(a)
+        result = sb.tile([P, T], F32, name="result", tag="key_words_then_old")
+        nc.sync.dma_start(out=result[:], in_=old)
 
-        pa = sb.tile([P, I], F32, name="pa")
-        runs = I // P
-        dealt = sb.tile([P, runs, P], F32, name="dealt")
-        for h in range(I // KCH):
-            nc.scalar.activation(out=dealt[:, :, h * KCH // runs:(h + 1) * KCH // runs], in_=a_ps[h][:].rearrange("p (m r) -> p r m", r=runs), func=ACT.Exp, bias=nm[:, h:h + 1])
-        cast(go_raw, two_g[:, PACK * Q:])
-        turned = ps.tile([P, P], F32, name="turned", tag="turned")
-        for j in range(runs):
-            nc.tensor.matmul(turned[:], lhsT=dealt[:, j, :], rhs=ident[:], is_transpose=True, start=(j == 0), stop=(j == runs - 1))
-        halves_t = sb.tile([P, P], F32, name="halves_t")
-        nc.scalar.copy(out=halves_t[:], in_=turned[:])
-        halves = ps.tile([P, P], F32, name="halves", tag="x")
-        nc.tensor.transpose(halves[:], halves_t[:], ident[:])
-        pg_c, pg_s = quant(pg_g[:], "pg")
-        pq_c, pq_s = quant(two_g[:, 0:PACK * Q], "pq")
-        go_c, go_s = quant(two_g[:, PACK * Q:], "go")
-        b_ps = ps.tile([P, U], F32, name="b")
-        mx(b_ps[:], pq_c[:], pq_s[:], pg_c[:], pg_s[:])
-        nmb = sb.tile([P, 1], F32, name="nmb")
-        nc.vector.tensor_reduce(out=nmb[:], in_=b_ps[:], axis=AX.X, op=ALU.max, negate=True)
+        neg_max = sb.tile([P, I // HALF], F32, name="neg_max")
+        for h in range(I // HALF):
+            nc.vector.tensor_reduce(out=neg_max[:, h:h + 1], in_=scores[h][:], axis=AX.X, op=ALU.max, negate=True)
+
+        dealt = shared.tile([P, RUN, P], F32, name="dealt", offset=AT_DEALT)
+        for h in range(I // HALF):
+            nc.scalar.activation(out=dealt[:, :, h * HALF // RUN:(h + 1) * HALF // RUN], in_=scores[h][:].rearrange("p (m r) -> p r m", r=RUN), func=ACT.Exp, bias=neg_max[:, h:h + 1])
+        turned = ps.tile([P, P], F32, name="turned", tag="turned_then_dp0")
+        for r in range(RUN):
+            nc.tensor.matmul(turned[:], lhsT=dealt[:, r, :], rhs=ident[:], is_transpose=True, start=(r == 0), stop=(r == RUN - 1))
+        turned_sb = sb.tile([P, P], F32, name="turned_sb")
+        nc.scalar.copy(out=turned_sb[:], in_=turned[:])
+        run_sums = ps.tile([P, P], F32, name="run_sums", tag="run_sums_then_dp1")
+        nc.tensor.transpose(run_sums[:], turned_sb[:], ident[:])
+
+        pa = shared.tile([P, I], F32, name="pa", offset=AT_PA)
+        for h in range(I // HALF):
+            nc.scalar.activation(out=pa[:, h * HALF:(h + 1) * HALF], in_=scores[h][:], func=ACT.Exp, bias=neg_max[:, h:h + 1])
+
+        pgsum_codes, pgsum_scales = quantize(pgsum_bf[:], "pgsum")
+        pair_codes, pair_scales = quantize(pair_bf[:], "pair")
+        b = ps.tile([P, U], F32, name="b")
+        product(b[:], pair_codes[:, 0:Q], pair_scales[:, 0:Q], pgsum_codes[:], pgsum_scales[:])
+        neg_max_b = sb.tile([P, 1], F32, name="neg_max_b")
+        nc.vector.tensor_reduce(out=neg_max_b[:], in_=b[:], axis=AX.X, op=ALU.max, negate=True)
         pb = sb.tile([P, U], F32, name="pb")
-        sb_sum = sb.tile([P, 1], F32, name="sb_sum")
-        nc.scalar.activation(out=pb[:], in_=b_ps[:], func=ACT.Exp, bias=nmb[:], accum_out=sb_sum[:])
-        rb = sb.tile([P, 1], F32, name="rb")
-        nc.vector.reciprocal(out=rb[:], in_=sb_sum[:])
+        sum_b = sb.tile([P, 1], F32, name="sum_b")
+        nc.scalar.activation(out=pb[:], in_=b[:], func=ACT.Exp, bias=neg_max_b[:], accum_out=sum_b[:])
+        inv_sum_b = sb.tile([P, 1], F32, name="inv_sum_b")
+        nc.vector.reciprocal(out=inv_sum_b[:], in_=sum_b[:])
         mb = sb.tile([P, U], F32, name="mb")
-        nc.scalar.activation(out=mb[:], in_=pb[:], func=ACT.Copy, scale=rb[:])
+        nc.scalar.activation(out=mb[:], in_=pb[:], func=ACT.Copy, scale=inv_sum_b[:])
         mg = sb.tile([P, G], F32, name="mg")
         nc.vector.tensor_tensor(out=mg[:], in0=mb[:].indirect(offs2_t[:]), in1=gain[:], op=ALU.mult)
 
-        s0 = sb.tile([P, G], F32, name="s0", tag="late")
-        zi = sb.tile([P, G], F32, name="zi")
+        s0 = sb.tile([P, G], F32, name="s0", tag="s0_then_products")
+        inv_s0 = sb.tile([P, G], F32, name="inv_s0")
         cf = sb.tile([P, G], F32, name="cf")
-        kf = sb.tile([P, G], F32, name="kf")
-        for h in range(I // KCH):
-            nc.scalar.activation(out=pa[:, h * KCH:(h + 1) * KCH], in_=a_ps[h][:], func=ACT.Exp, bias=nm[:, h:h + 1])
-        nc.vector.tensor_reduce(out=s0[:], in_=halves[:].rearrange("p (g j) -> p g j", j=PAGE // runs), axis=AX.X, op=ALU.add)
-        nc.vector.reciprocal(out=zi[:], in_=s0[:])
-        nc.gpsimd.tensor_tensor(out=cf[:], in0=zi[:], in1=mg[:], op=ALU.mult)
-        nc.gpsimd.tensor_tensor(out=kf[:], in0=cf[:], in1=zi[:], op=ALU.mult)
+        cf_over_s0 = sb.tile([P, G], F32, name="cf_over_s0")
+        nc.vector.tensor_reduce(out=s0[:], in_=run_sums[:].rearrange("p (g j) -> p g j", j=PAGE // RUN), axis=AX.X, op=ALU.add)
+        nc.vector.reciprocal(out=inv_s0[:], in_=s0[:])
+        nc.gpsimd.tensor_tensor(out=cf[:], in0=inv_s0[:], in1=mg[:], op=ALU.mult)
+        nc.gpsimd.tensor_tensor(out=cf_over_s0[:], in0=cf[:], in1=inv_s0[:], op=ALU.mult)
 
-        starts = [sum(VCHUNKS[:k]) for k in range(len(VCHUNKS))]
-        dp_ps = []
-        for k, (lo, n) in enumerate(zip(starts, VCHUNKS)):
-            vwg = sb.tile([P, n], U32, name="vwg%d" % k, align_bytes=64)
-            gather(vwg, vw, lo, n)
-            dp = ps.tile([P, n], F32, name="dp%d" % k, tag="x" if k == len(VCHUNKS) - 1 else "dp%d" % k)
-            mx(dp[:], go_c[:], go_s[:], vwg[:], vsg[:, lo:lo + n])
-            dp_ps.append(dp)
+        listed_val_scales = sb.tile([P, I], U8, name="listed_val_scales", tag="listed1", align_bytes=64)
+        gather(listed_val_scales, val_scales, 0, I)
+        chunks = [(sum(CHUNKS[:k]), n) for k, n in enumerate(CHUNKS)]
+        dp_tags = ("turned_then_dp0", "run_sums_then_dp1", "dp2")
+        dps = []
+        for k, (lo, n) in enumerate(chunks):
+            listed_val_words = sb.tile([P, n], U32, name="listed_val_words%d" % k, align_bytes=64)
+            gather(listed_val_words, val_words, lo, n)
+            dp = ps.tile([P, n], F32, name="dp%d" % k, tag=dp_tags[k])
+            product(dp[:], pair_codes[:, Q:], pair_scales[:, Q:], listed_val_words[:], listed_val_scales[:, lo:lo + n])
+            dps.append(dp)
 
-        s1 = sb.tile([P, G], F32, name="s1")
-        nb = sb.tile([P, G], F32, name="nb")
+        neg_s1 = sb.tile([P, G], F32, name="neg_s1")
+        shift = sb.tile([P, G], F32, name="shift")
+        first_products = sb.tile([P, CHUNKS[0]], F32, name="first_products")
+        later_products = sb.tile([P, I - CHUNKS[0]], F32, name="later_products", tag="s0_then_products")
         ws = []
-        e_first = sb.tile([P, VCHUNKS[0]], F32, name="e_first")
-        e_rest = sb.tile([P, I - VCHUNKS[0]], F32, name="e_rest", tag="late")
-        for k, (lo, n) in enumerate(zip(starts, VCHUNKS)):
-            gs = slice(lo // PAGE, (lo + n) // PAGE)
-            e = e_first[:] if k == 0 else e_rest[:, lo - VCHUNKS[0]:lo - VCHUNKS[0] + n]
-            nc.vector.tensor_tensor(out=e, in0=dp_ps[k][:], in1=pa[:, lo:lo + n], op=ALU.mult)
-            nc.vector.tensor_reduce(out=s1[:, gs], in_=e.rearrange("p (g j) -> p g j", j=PAGE), axis=AX.X, op=ALU.add, negate=True)
-            nc.gpsimd.tensor_tensor(out=nb[:, gs], in0=s1[:, gs], in1=kf[:, gs], op=ALU.mult)
+        for k, (lo, n) in enumerate(chunks):
+            pages = slice(lo // PAGE, (lo + n) // PAGE)
+            pa_dp = first_products[:] if k == 0 else later_products[:, lo - CHUNKS[0]:lo - CHUNKS[0] + n]
+            nc.vector.tensor_tensor(out=pa_dp, in0=dps[k][:], in1=pa[:, lo:lo + n], op=ALU.mult)
+            nc.vector.tensor_reduce(out=neg_s1[:, pages], in_=pa_dp.rearrange("p (g j) -> p g j", j=PAGE), axis=AX.X, op=ALU.add, negate=True)
+            nc.gpsimd.tensor_tensor(out=shift[:, pages], in0=neg_s1[:, pages], in1=cf_over_s0[:, pages], op=ALU.mult)
             w = sb.tile([P, n], F32, name="w%d" % k)
-            for g in range(n // PAGE):
-                gg = lo // PAGE + g
-                nc.scalar.activation(out=w[:, g * PAGE:(g + 1) * PAGE], in_=dp_ps[k][:, g * PAGE:(g + 1) * PAGE], func=ACT.Identity, scale=cf[:, gg:gg + 1], bias=nb[:, gg:gg + 1])
+            for j in range(n // PAGE):
+                g = lo // PAGE + j
+                nc.scalar.activation(out=w[:, j * PAGE:(j + 1) * PAGE], in_=dps[k][:, j * PAGE:(j + 1) * PAGE], func=ACT.Identity, scale=cf[:, g:g + 1], bias=shift[:, g:g + 1])
             ws.append(w)
-        for k, (lo, n) in enumerate(zip(starts, VCHUNKS)):
-            nc.vector.tensor_tensor(out=df[:].indirect(offs_t[:, lo // 16:(lo + n) // 16]), in0=pa[:, lo:lo + n], in1=ws[k][:], op=ALU.mult)
 
-        lo = 0
-        for c, width in enumerate((256, 512, 640, 640)):
-            cs = slice(lo, lo + width)
-            lo = lo + width
-            nc.vector.tensor_tensor(out=acc[:, cs], in0=acc[:, cs], in1=df[:, cs], op=ALU.add)
-            (nc.sync if c % 2 == 0 else nc.scalar).dma_start(out=out[:, cs], in_=acc[:, cs])
+        for k, (lo, n) in enumerate(chunks):
+            nc.vector.tensor_tensor(out=df[:].indirect(slots(lo, n)), in0=pa[:, lo:lo + n], in1=ws[k][:], op=ALU.mult)
+
+        for c, width in enumerate(STORES):
+            cols = slice(sum(STORES[:c]), sum(STORES[:c]) + width)
+            nc.vector.tensor_tensor(out=result[:, cols], in0=result[:, cols], in1=df[:, cols], op=ALU.add)
+            queue = nc.sync if c % 2 == 0 else nc.scalar
+            queue.dma_start(out=out[:, cols], in_=result[:, cols])

@@ -27,13 +27,12 @@ RUN = I // P
 CHUNKS = (256, 256, 512)
 STORES = (256, 512, 640, 640)
 
-AT_PA = 1024
-AT_QUERY = 4096
-QUERY_STAGE = 1280
-AT_GOUT = 4096
-AT_DEALT = 5120
-AT_PQUERY = 6144
-AT_PGSUM = 8192
+AT_KEY_WORDS = 0
+AT_GOUT = AT_KEY_WORDS + 4 * T
+AT_PQUERY = AT_GOUT + 4 * PACK * Q
+AT_PGSUM = AT_PQUERY + 4 * PACK * Q
+AT_QUERY = AT_GOUT - 1024
+QUERY_STAGE = (AT_PGSUM + 512 - AT_QUERY) // 4
 
 
 def tile_attend_gwithinpage_kernel(tc, query, keys_words, keys_scales, pquery, pgsum, gout, vals_words, vals_scales, old, offs, offs2, out):
@@ -81,13 +80,11 @@ def tile_attend_gwithinpage_kernel(tc, query, keys_words, keys_scales, pquery, p
             nc.tensor.matmul_mx(out=acc, lhsT=lhs_codes.bitcast(FP8X4), lhsT_scale=lhs_scales, rhs=rhs_codes.bitcast(FP8X4), rhs_scale=rhs_scales, start=True, stop=True)
 
         nc.sync.dma_start(offs_t[:], offs)
-        nc.sync.dma_start(offs2_t[:], offs2)
         query_stage = shared.tile([P, QUERY_STAGE], F32, name="query_stage", offset=AT_QUERY)
         query_rows = load_rows(query, query_stage[:, 0:PACK * Q])
+        nc.sync.dma_start(offs2_t[:], offs2)
         key_scales = sb.tile([P, T], U8, name="key_scales", tag="key_scales_then_val_words")
         load_scales(keys_scales, key_scales)
-        key_words = sb.tile([P, T], U32, name="key_words", tag="key_words_then_old")
-        load_words(keys_words, key_words)
         val_scales = sb.tile([P, T], U8, name="val_scales")
         load_scales(vals_scales, val_scales)
         df = sb.tile([P, T], F32, name="df")
@@ -99,6 +96,8 @@ def tile_attend_gwithinpage_kernel(tc, query, keys_words, keys_scales, pquery, p
 
         query_bf = sb.tile([P, PACK * Q], BF16, name="query_bf", align_bytes=64)
         interleave(query_rows, query_bf[:])
+        key_words = shared.tile([P, T], U32, name="key_words", offset=AT_KEY_WORDS)
+        load_words(keys_words, key_words)
         pgsum_stage = shared.tile([P, PACK * U], F32, name="pgsum_stage", offset=AT_PGSUM)
         pgsum_rows = load_rows(pgsum, pgsum_stage[:])
         pquery_stage = shared.tile([P, PACK * Q], F32, name="pquery_stage", offset=AT_PQUERY)
@@ -111,46 +110,46 @@ def tile_attend_gwithinpage_kernel(tc, query, keys_words, keys_scales, pquery, p
         val_words = sb.tile([P, T], U32, name="val_words", tag="key_scales_then_val_words")
         load_words(vals_words, val_words)
         query_codes, query_scales = quantize(query_bf[:], "query")
+        listed_val_scales = sb.tile([P, I], U8, name="listed_val_scales", align_bytes=64)
+        gather(listed_val_scales, val_scales, 0, I)
 
         pair_bf = sb.tile([P, PACK * 2 * Q], BF16, name="pair_bf", align_bytes=64)
         pgsum_bf = sb.tile([P, PACK * U], BF16, name="pgsum_bf", align_bytes=64)
         interleave(pgsum_rows, pgsum_bf[:])
         interleave(pquery_rows, pair_bf[:, 0:PACK * Q])
-        interleave(gout_rows, pair_bf[:, PACK * Q:])
 
         scores = []
         for h in range(I // HALF):
-            listed_key_words = sb.tile([P, HALF], U32, name="listed_key_words%d" % h, tag="listed%d" % h, align_bytes=64)
+            listed_key_words = sb.tile([P, HALF], U32, name="listed_key_words%d" % h, align_bytes=64)
             gather(listed_key_words, key_words, h * HALF, HALF)
             a = ps.tile([P, HALF], F32, name="a%d" % h)
             product(a[:], query_codes[:], query_scales[:], listed_key_words[:], listed_key_scales[:, h * HALF:(h + 1) * HALF])
             scores.append(a)
-        result = sb.tile([P, T], F32, name="result", tag="key_words_then_old")
+        result = shared.tile([P, T], F32, name="result", offset=AT_KEY_WORDS)
         nc.sync.dma_start(out=result[:], in_=old)
 
         neg_max = sb.tile([P, I // HALF], F32, name="neg_max")
         for h in range(I // HALF):
             nc.vector.tensor_reduce(out=neg_max[:, h:h + 1], in_=scores[h][:], axis=AX.X, op=ALU.max, negate=True)
 
-        dealt = shared.tile([P, RUN, P], F32, name="dealt", offset=AT_DEALT)
+        pa = sb.tile([P, I], F32, name="pa")
+        dealt = sb.tile([P, RUN, P], F32, name="dealt")
         for h in range(I // HALF):
             nc.scalar.activation(out=dealt[:, :, h * HALF // RUN:(h + 1) * HALF // RUN], in_=scores[h][:].rearrange("p (m r) -> p r m", r=RUN), func=ACT.Exp, bias=neg_max[:, h:h + 1])
-        turned = ps.tile([P, P], F32, name="turned", tag="turned_then_dp0")
+        interleave(gout_rows, pair_bf[:, PACK * Q:])
+        turned = ps.tile([P, P], F32, name="turned")
         for r in range(RUN):
             nc.tensor.matmul(turned[:], lhsT=dealt[:, r, :], rhs=ident[:], is_transpose=True, start=(r == 0), stop=(r == RUN - 1))
         turned_sb = sb.tile([P, P], F32, name="turned_sb")
         nc.scalar.copy(out=turned_sb[:], in_=turned[:])
-        run_sums = ps.tile([P, P], F32, name="run_sums", tag="run_sums_then_dp1")
+        run_sums = ps.tile([P, P], F32, name="run_sums", tag="run_sums_then_last_dp")
         nc.tensor.transpose(run_sums[:], turned_sb[:], ident[:])
 
-        pa = shared.tile([P, I], F32, name="pa", offset=AT_PA)
-        for h in range(I // HALF):
-            nc.scalar.activation(out=pa[:, h * HALF:(h + 1) * HALF], in_=scores[h][:], func=ACT.Exp, bias=neg_max[:, h:h + 1])
-
         pgsum_codes, pgsum_scales = quantize(pgsum_bf[:], "pgsum")
-        pair_codes, pair_scales = quantize(pair_bf[:], "pair")
+        pquery_codes, pquery_scales = quantize(pair_bf[:, 0:PACK * Q], "pquery")
+        gout_codes, gout_scales = quantize(pair_bf[:, PACK * Q:], "gout")
         b = ps.tile([P, U], F32, name="b")
-        product(b[:], pair_codes[:, 0:Q], pair_scales[:, 0:Q], pgsum_codes[:], pgsum_scales[:])
+        product(b[:], pquery_codes[:], pquery_scales[:], pgsum_codes[:], pgsum_scales[:])
         neg_max_b = sb.tile([P, 1], F32, name="neg_max_b")
         nc.vector.tensor_reduce(out=neg_max_b[:], in_=b[:], axis=AX.X, op=ALU.max, negate=True)
         pb = sb.tile([P, U], F32, name="pb")
@@ -166,25 +165,24 @@ def tile_attend_gwithinpage_kernel(tc, query, keys_words, keys_scales, pquery, p
         s0 = sb.tile([P, G], F32, name="s0", tag="s0_then_products")
         inv_s0 = sb.tile([P, G], F32, name="inv_s0")
         cf = sb.tile([P, G], F32, name="cf")
-        cf_over_s0 = sb.tile([P, G], F32, name="cf_over_s0")
+        for h in range(I // HALF):
+            nc.scalar.activation(out=pa[:, h * HALF:(h + 1) * HALF], in_=scores[h][:], func=ACT.Exp, bias=neg_max[:, h:h + 1])
         nc.vector.tensor_reduce(out=s0[:], in_=run_sums[:].rearrange("p (g j) -> p g j", j=PAGE // RUN), axis=AX.X, op=ALU.add)
         nc.vector.reciprocal(out=inv_s0[:], in_=s0[:])
         nc.gpsimd.tensor_tensor(out=cf[:], in0=inv_s0[:], in1=mg[:], op=ALU.mult)
-        nc.gpsimd.tensor_tensor(out=cf_over_s0[:], in0=cf[:], in1=inv_s0[:], op=ALU.mult)
 
-        listed_val_scales = sb.tile([P, I], U8, name="listed_val_scales", tag="listed1", align_bytes=64)
-        gather(listed_val_scales, val_scales, 0, I)
         chunks = [(sum(CHUNKS[:k]), n) for k, n in enumerate(CHUNKS)]
-        dp_tags = ("turned_then_dp0", "run_sums_then_dp1", "dp2")
+        dp_tags = ("dp0", "dp1", "run_sums_then_last_dp")
         dps = []
         for k, (lo, n) in enumerate(chunks):
             listed_val_words = sb.tile([P, n], U32, name="listed_val_words%d" % k, align_bytes=64)
             gather(listed_val_words, val_words, lo, n)
             dp = ps.tile([P, n], F32, name="dp%d" % k, tag=dp_tags[k])
-            product(dp[:], pair_codes[:, Q:], pair_scales[:, Q:], listed_val_words[:], listed_val_scales[:, lo:lo + n])
+            product(dp[:], gout_codes[:], gout_scales[:], listed_val_words[:], listed_val_scales[:, lo:lo + n])
             dps.append(dp)
 
         neg_s1 = sb.tile([P, G], F32, name="neg_s1")
+        neg_md = sb.tile([P, G], F32, name="neg_md")
         shift = sb.tile([P, G], F32, name="shift")
         first_products = sb.tile([P, CHUNKS[0]], F32, name="first_products")
         later_products = sb.tile([P, I - CHUNKS[0]], F32, name="later_products", tag="s0_then_products")
@@ -194,7 +192,8 @@ def tile_attend_gwithinpage_kernel(tc, query, keys_words, keys_scales, pquery, p
             pa_dp = first_products[:] if k == 0 else later_products[:, lo - CHUNKS[0]:lo - CHUNKS[0] + n]
             nc.vector.tensor_tensor(out=pa_dp, in0=dps[k][:], in1=pa[:, lo:lo + n], op=ALU.mult)
             nc.vector.tensor_reduce(out=neg_s1[:, pages], in_=pa_dp.rearrange("p (g j) -> p g j", j=PAGE), axis=AX.X, op=ALU.add, negate=True)
-            nc.gpsimd.tensor_tensor(out=shift[:, pages], in0=neg_s1[:, pages], in1=cf_over_s0[:, pages], op=ALU.mult)
+            nc.gpsimd.tensor_tensor(out=neg_md[:, pages], in0=neg_s1[:, pages], in1=inv_s0[:, pages], op=ALU.mult)
+            nc.gpsimd.tensor_tensor(out=shift[:, pages], in0=neg_md[:, pages], in1=cf[:, pages], op=ALU.mult)
             w = sb.tile([P, n], F32, name="w%d" % k)
             for j in range(n // PAGE):
                 g = lo // PAGE + j

from contextlib import ExitStack

import concourse.mybir as mybir
from concourse.masks import make_identity

D, E, T, I, G, U, Q = 512, 512, 2048, 1024, 64, 256, 128
FLOPS = 2 * Q * (D * U + D * I + E * I)

F32 = mybir.dt.float32
BF16 = mybir.dt.bfloat16
I32 = mybir.dt.int32
U32 = mybir.dt.uint32
U16 = mybir.dt.uint16
U8 = mybir.dt.uint8
FP8X4 = mybir.dt.float8_e4m3fn_x4
ALU = mybir.AluOpType
ACT = mybir.ActivationFunctionType
AX = mybir.AxisListType

P = 128
PACK = 4
PAGE = I // G
PER_COLUMN = 16
HALF = 512
RUN = I // P

CHUNKS = (256, 256, 512)
STORES = (256, 512, 640, 640)

AT_KEY_WORDS = 0
AT_GOUT = AT_KEY_WORDS + 4 * T
AT_PQUERY = AT_GOUT + 4 * PACK * Q
AT_PGSUM = AT_PQUERY + 4 * PACK * Q
AT_QUERY = AT_GOUT - 1024
QUERY_STAGE = (AT_PGSUM + 512 - AT_QUERY) // 4


def tile_attend_gwithinpage_kernel(tc, query, keys_words, keys_scales, pquery, pgsum, gout, vals_words, vals_scales, old, offs, offs2, out):
    nc = tc.nc
    with ExitStack() as ctx:
        lists = ctx.enter_context(tc.tile_pool(name="lists", bufs=1))
        sb = ctx.enter_context(tc.tile_pool(name="sb", bufs=1))
        shared = ctx.enter_context(tc.tile_pool(name="shared", bufs=1))
        ps = ctx.enter_context(tc.psum_pool(name="ps", bufs=1))

        offs_t = lists.tile([P, I // PER_COLUMN], U16, name="offs_t")
        offs2_t = lists.tile([P, G // PER_COLUMN], U16, name="offs2_t")

        def slots(lo, n):
            return offs_t[:, lo // PER_COLUMN:(lo + n) // PER_COLUMN]

        def load_rows(src, flat):
            rows = flat.rearrange("p (t w) -> p t w", t=PACK)
            nc.sync.dma_start(out=rows, in_=src.rearrange("(p t) w -> p t w", t=PACK))
            return rows

        def load_words(src, window):
            nc.sync.dma_start(out=window[:].bitcast(I32), in_=src[0].rearrange("p n t -> p (n t)").bitcast(I32))

        def load_scales(src, window):
            nc.vector.memset(window[:, 0:T // 2].bitcast(I32), 0)
            nc.gpsimd.memset(window[:, T // 2:].bitcast(I32), 0)
            for r in range(4):
                nc.sync.dma_start(out=window[r:P:32, :].bitcast(I32), in_=src[0, r:16:4, :].bitcast(I32))

        def interleave(rows, grouped):
            nc.scalar.activation(out=grouped.rearrange("p (c i t) -> p c t i", i=4, t=PACK), in_=rows.rearrange("p t (c i) -> p c t i", i=4), func=ACT.Copy)

        def quantize(grouped, name):
            width = grouped.shape[1] // PACK
            codes = sb.tile([P, width], U32, name=name + "_codes", align_bytes=64)
            scales = sb.tile([P, width], U8, name=name + "_scales", align_bytes=64)
            nc.vector.quantize_mx(out=codes[:].bitcast(FP8X4), scales=scales[:], in_=grouped)
            return codes, scales

        def gather(dst, window, lo, n):
            nc.vector.tensor_copy(out=dst[:], in_=window[:].indirect(slots(lo, n)))

        def product(acc, lhs_codes, lhs_scales, rhs_codes, rhs_scales):
            nc.tensor.matmul_mx(out=acc, lhsT=lhs_codes.bitcast(FP8X4), lhsT_scale=lhs_scales, rhs=rhs_codes.bitcast(FP8X4), rhs_scale=rhs_scales, start=True, stop=True)

        nc.sync.dma_start(offs_t[:], offs)
        query_stage = shared.tile([P, QUERY_STAGE], F32, name="query_stage", offset=AT_QUERY)
        query_rows = load_rows(query, query_stage[:, 0:PACK * Q])
        nc.sync.dma_start(offs2_t[:], offs2)
        key_scales = sb.tile([P, T], U8, name="key_scales", tag="key_scales_then_val_words")
        load_scales(keys_scales, key_scales)
        val_scales = sb.tile([P, T], U8, name="val_scales")
        load_scales(vals_scales, val_scales)
        df = sb.tile([P, T], F32, name="df")
        nc.vector.memset(df[:], 0.0)
        ident = sb.tile([P, P], F32, name="ident")
        make_identity(nc, ident[:])
        gain = sb.tile([P, G], F32, name="gain")
        nc.gpsimd.memset(gain[:], 256.0)

        query_bf = sb.tile([P, PACK * Q], BF16, name="query_bf", align_bytes=64)
        interleave(query_rows, query_bf[:])
        key_words = shared.tile([P, T], U32, name="key_words", offset=AT_KEY_WORDS)
        load_words(keys_words, key_words)
        pgsum_stage = shared.tile([P, PACK * U], F32, name="pgsum_stage", offset=AT_PGSUM)
        pgsum_rows = load_rows(pgsum, pgsum_stage[:])
        pquery_stage = shared.tile([P, PACK * Q], F32, name="pquery_stage", offset=AT_PQUERY)
        pquery_rows = load_rows(pquery, pquery_stage[:])
        gout_stage = shared.tile([P, PACK * Q], F32, name="gout_stage", offset=AT_GOUT)
        gout_rows = load_rows(gout, gout_stage[:])

        listed_key_scales = sb.tile([P, I], U8, name="listed_key_scales", align_bytes=64)
        gather(listed_key_scales, key_scales, 0, I)
        val_words = sb.tile([P, T], U32, name="val_words", tag="key_scales_then_val_words")
        load_words(vals_words, val_words)
        query_codes, query_scales = quantize(query_bf[:], "query")
        listed_val_scales = sb.tile([P, I], U8, name="listed_val_scales", align_bytes=64)
        gather(listed_val_scales, val_scales, 0, I)

        pair_bf = sb.tile([P, PACK * 2 * Q], BF16, name="pair_bf", align_bytes=64)
        pgsum_bf = sb.tile([P, PACK * U], BF16, name="pgsum_bf", align_bytes=64)
        interleave(pgsum_rows, pgsum_bf[:])
        interleave(pquery_rows, pair_bf[:, 0:PACK * Q])

        scores = []
        for h in range(I // HALF):
            listed_key_words = sb.tile([P, HALF], U32, name="listed_key_words%d" % h, align_bytes=64)
            gather(listed_key_words, key_words, h * HALF, HALF)
            a = ps.tile([P, HALF], F32, name="a%d" % h)
            product(a[:], query_codes[:], query_scales[:], listed_key_words[:], listed_key_scales[:, h * HALF:(h + 1) * HALF])
            scores.append(a)
        result = shared.tile([P, T], F32, name="result", offset=AT_KEY_WORDS)
        nc.sync.dma_start(out=result[:], in_=old)

        neg_max = sb.tile([P, I // HALF], F32, name="neg_max")
        for h in range(I // HALF):
            nc.vector.tensor_reduce(out=neg_max[:, h:h + 1], in_=scores[h][:], axis=AX.X, op=ALU.max, negate=True)

        pa = sb.tile([P, I], F32, name="pa")
        dealt = sb.tile([P, RUN, P], F32, name="dealt")
        for h in range(I // HALF):
            nc.scalar.activation(out=dealt[:, :, h * HALF // RUN:(h + 1) * HALF // RUN], in_=scores[h][:].rearrange("p (m r) -> p r m", r=RUN), func=ACT.Exp, bias=neg_max[:, h:h + 1])
        interleave(gout_rows, pair_bf[:, PACK * Q:])
        turned = ps.tile([P, P], F32, name="turned")
        for r in range(RUN):
            nc.tensor.matmul(turned[:], lhsT=dealt[:, r, :], rhs=ident[:], is_transpose=True, start=(r == 0), stop=(r == RUN - 1))
        turned_sb = sb.tile([P, P], F32, name="turned_sb")
        nc.scalar.copy(out=turned_sb[:], in_=turned[:])
        run_sums = ps.tile([P, P], F32, name="run_sums", tag="run_sums_then_last_dp")
        nc.tensor.transpose(run_sums[:], turned_sb[:], ident[:])

        pgsum_codes, pgsum_scales = quantize(pgsum_bf[:], "pgsum")
        pquery_codes, pquery_scales = quantize(pair_bf[:, 0:PACK * Q], "pquery")
        gout_codes, gout_scales = quantize(pair_bf[:, PACK * Q:], "gout")
        b = ps.tile([P, U], F32, name="b")
        product(b[:], pquery_codes[:], pquery_scales[:], pgsum_codes[:], pgsum_scales[:])
        neg_max_b = sb.tile([P, 1], F32, name="neg_max_b")
        nc.vector.tensor_reduce(out=neg_max_b[:], in_=b[:], axis=AX.X, op=ALU.max, negate=True)
        pb = sb.tile([P, U], F32, name="pb")
        sum_b = sb.tile([P, 1], F32, name="sum_b")
        nc.scalar.activation(out=pb[:], in_=b[:], func=ACT.Exp, bias=neg_max_b[:], accum_out=sum_b[:])
        inv_sum_b = sb.tile([P, 1], F32, name="inv_sum_b")
        nc.vector.reciprocal(out=inv_sum_b[:], in_=sum_b[:])
        mb = sb.tile([P, U], F32, name="mb")
        nc.scalar.activation(out=mb[:], in_=pb[:], func=ACT.Copy, scale=inv_sum_b[:])
        mg = sb.tile([P, G], F32, name="mg")
        nc.vector.tensor_tensor(out=mg[:], in0=mb[:].indirect(offs2_t[:]), in1=gain[:], op=ALU.mult)

        s0 = sb.tile([P, G], F32, name="s0", tag="s0_then_products")
        inv_s0 = sb.tile([P, G], F32, name="inv_s0")
        cf = sb.tile([P, G], F32, name="cf")
        for h in range(I // HALF):
            nc.scalar.activation(out=pa[:, h * HALF:(h + 1) * HALF], in_=scores[h][:], func=ACT.Exp, bias=neg_max[:, h:h + 1])
        nc.vector.tensor_reduce(out=s0[:], in_=run_sums[:].rearrange("p (g j) -> p g j", j=PAGE // RUN), axis=AX.X, op=ALU.add)
        nc.vector.reciprocal(out=inv_s0[:], in_=s0[:])
        nc.gpsimd.tensor_tensor(out=cf[:], in0=inv_s0[:], in1=mg[:], op=ALU.mult)

        chunks = [(sum(CHUNKS[:k]), n) for k, n in enumerate(CHUNKS)]
        dp_tags = ("dp0", "dp1", "run_sums_then_last_dp")
        dps = []
        for k, (lo, n) in enumerate(chunks):
            listed_val_words = sb.tile([P, n], U32, name="listed_val_words%d" % k, align_bytes=64)
            gather(listed_val_words, val_words, lo, n)
            dp = ps.tile([P, n], F32, name="dp%d" % k, tag=dp_tags[k])
            product(dp[:], gout_codes[:], gout_scales[:], listed_val_words[:], listed_val_scales[:, lo:lo + n])
            dps.append(dp)

        neg_s1 = sb.tile([P, G], F32, name="neg_s1")
        neg_md = sb.tile([P, G], F32, name="neg_md")
        shift = sb.tile([P, G], F32, name="shift")
        first_products = sb.tile([P, CHUNKS[0]], F32, name="first_products")
        later_products = sb.tile([P, I - CHUNKS[0]], F32, name="later_products", tag="s0_then_products")
        ws = []
        for k, (lo, n) in enumerate(chunks):
            pages = slice(lo // PAGE, (lo + n) // PAGE)
            pa_dp = first_products[:] if k == 0 else later_products[:, lo - CHUNKS[0]:lo - CHUNKS[0] + n]
            nc.vector.tensor_tensor(out=pa_dp, in0=dps[k][:], in1=pa[:, lo:lo + n], op=ALU.mult)
            nc.vector.tensor_reduce(out=neg_s1[:, pages], in_=pa_dp.rearrange("p (g j) -> p g j", j=PAGE), axis=AX.X, op=ALU.add, negate=True)
            nc.gpsimd.tensor_tensor(out=neg_md[:, pages], in0=neg_s1[:, pages], in1=inv_s0[:, pages], op=ALU.mult)
            nc.gpsimd.tensor_tensor(out=shift[:, pages], in0=neg_md[:, pages], in1=cf[:, pages], op=ALU.mult)
            w = sb.tile([P, n], F32, name="w%d" % k)
            for j in range(n // PAGE):
                g = lo // PAGE + j
                nc.scalar.activation(out=w[:, j * PAGE:(j + 1) * PAGE], in_=dps[k][:, j * PAGE:(j + 1) * PAGE], func=ACT.Identity, scale=cf[:, g:g + 1], bias=shift[:, g:g + 1])
            ws.append(w)

        for k, (lo, n) in enumerate(chunks):
            nc.vector.tensor_tensor(out=df[:].indirect(slots(lo, n)), in0=pa[:, lo:lo + n], in1=ws[k][:], op=ALU.mult)

        for c, width in enumerate(STORES):
            cols = slice(sum(STORES[:c]), sum(STORES[:c]) + width)
            nc.vector.tensor_tensor(out=result[:, cols], in0=result[:, cols], in1=df[:, cols], op=ALU.add)
            queue = nc.sync if c % 2 == 0 else nc.scalar
            queue.dma_start(out=out[:, cols], in_=result[:, cols])
